import numpy as np
import ml_dtypes

BF16 = ml_dtypes.bfloat16


def bf(x):
    return np.asarray(x, np.float32).astype(BF16)


def f32(x):
    return np.asarray(x, np.float32)


def f64(x):
    return np.asarray(x).astype(np.float64)


def striped(idx):
    return np.tile(idx.reshape(-1, 16).T, (8, 1))


def rows(idx, k):
    return np.tile(idx, (k, 1))


def look(tab, idx):
    return np.take_along_axis(f64(tab), rows(idx, len(tab)), axis=1)


K, S, V, N, M = 256, 2048, 512, 512, 128


def setup_inputs():
    return {"tab": f32(np.random.standard_normal((2, K, S))), "y": f32(np.random.standard_normal((K, V))), "w": bf(np.random.standard_normal((K, M)) / np.sqrt(K)), "b": f32(0.5 * np.random.standard_normal((M, 1))), "offs": striped(np.random.permutation(S)[:N])}


def reference(tab, y, w, b, offs):
    idx = offs[:16].T.reshape(-1)
    x = (look(tab[0], idx) * f64(y)) * (np.tanh(look(tab[1], idx)))
    return np.maximum(f64(w).T @ x + f64(b), 0.0)

@@ -1,0 +1,58 @@
+import concourse.mybir as mybir
+
+F32, BF16, U16 = mybir.dt.float32, mybir.dt.bfloat16, mybir.dt.uint16
+mult = mybir.AluOpType.mult
+tanh = mybir.ActivationFunctionType.Tanh
+relu = mybir.ActivationFunctionType.Relu
+
+P = 128
+K, S, N, M = 256, 2048, 512, 128
+BLOCKS = K // P
+PIECES = 2
+C = N // PIECES
+
+FLOPS = 2 * K * M * N + 2 * K * N
+
+
+def tile_lookup_vg_multanh_relu_kernel(tc, tab, y, w, b, offs, out):
+    nc = tc.nc
+    with (
+        tc.tile_pool(name="held", bufs=1) as held,
+        tc.psum_pool(name="psum", bufs=1) as psum,
+    ):
+        offsets = held.tile([P, N // 16], U16, name="offsets")
+        values = [held.tile([P, S], F32, name=f"values{k}") for k in range(BLOCKS)]
+        gates = [held.tile([P, S], F32, name=f"gates{k}") for k in range(BLOCKS)]
+        stream = held.tile([P, BLOCKS, N], F32, name="stream")
+        weights = held.tile([P, BLOCKS, M], BF16, name="weights")
+        bias = held.tile([P, 1], F32, name="bias")
+
+        nc.sync.dma_start(offsets[:], offs)
+        nc.sync.dma_start(gates[0][:], tab[1, 0:P, :])
+        nc.sync.dma_start(stream[:], y.rearrange("(k p) n -> p k n", p=P))
+        nc.sync.dma_start(values[0][:], tab[0, 0:P, :])
+        nc.sync.dma_start(values[1][:], tab[0, P:K, :])
+        nc.sync.dma_start(gates[1][:], tab[1, P:K, :])
+        nc.scalar.dma_start(weights[:], w.rearrange("(k p) m -> p k m", p=P))
+        nc.scalar.dma_start(bias[:], b)
+
+        layer = [psum.tile([M, C], F32, name=f"layer{c}") for c in range(PIECES)]
+        for k in range(BLOCKS):
+            scaled = [held.tile([P, C], F32, name=f"scaled{k}_{c}") for c in range(PIECES)]
+            gate = [held.tile([P, C], F32, name=f"gate{k}_{c}") for c in range(PIECES)]
+            x = [held.tile([P, C], BF16, name=f"x{k}_{c}") for c in range(PIECES)]
+            for c in range(PIECES):
+                entries = offsets[:, c * C // 16 : (c + 1) * C // 16]
+                nc.vector.tensor_tensor(
+                    scaled[c][:], values[k][:].indirect(entries), stream[:, k, c * C : (c + 1) * C], mult
+                )
+            for c in range(PIECES):
+                entries = offsets[:, c * C // 16 : (c + 1) * C // 16]
+                nc.scalar.activation(gate[c][:], gates[k][:].indirect(entries), tanh)
+                nc.vector.tensor_tensor(x[c][:], scaled[c][:], gate[c][:], mult)
+                nc.tensor.matmul(layer[c][:], weights[:, k, :], x[c][:], start=k == 0, stop=k == BLOCKS - 1)
+
+        for c in range(PIECES):
+            result = held.tile([M, C], F32, name=f"result{c}")
+            nc.scalar.activation(result[:], layer[c][:], relu, bias=bias[:])
+            nc.sync.dma_start(out[:, c * C : (c + 1) * C], result[:])

@@ -1,14 +1,14 @@
 import concourse.mybir as mybir
 
 F32, BF16, U16 = mybir.dt.float32, mybir.dt.bfloat16, mybir.dt.uint16
-mult = mybir.AluOpType.mult
+mult, add, largest = mybir.AluOpType.mult, mybir.AluOpType.add, mybir.AluOpType.max
 tanh = mybir.ActivationFunctionType.Tanh
 relu = mybir.ActivationFunctionType.Relu
 
 P = 128
 K, S, N, M = 256, 2048, 512, 128
 BLOCKS = K // P
-PIECES = 2
+PIECES = 4
 C = N // PIECES
 
 FLOPS = 2 * K * M * N + 2 * K * N
@@ -29,12 +29,13 @@ def tile_lookup_vg_multanh_relu_kernel(tc, tab, y, w, b, offs, out):
 
         nc.sync.dma_start(offsets[:], offs)
         nc.sync.dma_start(gates[0][:], tab[1, 0:P, :])
-        nc.sync.dma_start(stream[:], y.rearrange("(k p) n -> p k n", p=P))
+        nc.sync.dma_start(stream[:, 0, :], y[0:P, :])
         nc.sync.dma_start(values[0][:], tab[0, 0:P, :])
+        nc.sync.dma_start(stream[:, 1, :], y[P:K, :])
         nc.sync.dma_start(values[1][:], tab[0, P:K, :])
         nc.sync.dma_start(gates[1][:], tab[1, P:K, :])
-        nc.scalar.dma_start(weights[:], w.rearrange("(k p) m -> p k m", p=P))
-        nc.scalar.dma_start(bias[:], b)
+        nc.sync.dma_start(weights[:], w.rearrange("(k p) m -> p k m", p=P))
+        nc.sync.dma_start(bias[:], b)
 
         layer = [psum.tile([M, C], F32, name=f"layer{c}") for c in range(PIECES)]
         for k in range(BLOCKS):
@@ -54,5 +55,8 @@ def tile_lookup_vg_multanh_relu_kernel(tc, tab, y, w, b, offs, out):
 
         for c in range(PIECES):
             result = held.tile([M, C], F32, name=f"result{c}")
-            nc.scalar.activation(result[:], layer[c][:], relu, bias=bias[:])
+            if c % 2 == 0:
+                nc.scalar.activation(result[:], layer[c][:], relu, bias=bias[:])
+            else:
+                nc.vector.tensor_scalar(result[:], layer[c][:], bias[:], 0.0, add, largest)
             nc.sync.dma_start(out[:, c * C : (c + 1) * C], result[:])

@@ -27,6 +27,8 @@ def tile_lookup_vg_multanh_relu_kernel(tc, tab, y, w, b, offs, out):
         weights = held.tile([P, BLOCKS, M], BF16, name="weights")
         bias = held.tile([P, 1], F32, name="bias")
 
+        nc.scalar.dma_start(weights[:], w.rearrange("(k p) m -> p k m", p=P))
+        nc.scalar.dma_start(bias[:], b)
         nc.sync.dma_start(offsets[:], offs)
         nc.sync.dma_start(gates[0][:], tab[1, 0:P, :])
         nc.sync.dma_start(stream[:, 0, :], y[0:P, :])
@@ -34,8 +36,6 @@ def tile_lookup_vg_multanh_relu_kernel(tc, tab, y, w, b, offs, out):
         nc.sync.dma_start(stream[:, 1, :], y[P:K, :])
         nc.sync.dma_start(values[1][:], tab[0, P:K, :])
         nc.sync.dma_start(gates[1][:], tab[1, P:K, :])
-        nc.sync.dma_start(weights[:], w.rearrange("(k p) m -> p k m", p=P))
-        nc.sync.dma_start(bias[:], b)
 
         layer = [psum.tile([M, C], F32, name=f"layer{c}") for c in range(PIECES)]
         for k in range(BLOCKS):

import concourse.mybir as mybir

F32, BF16, U16 = mybir.dt.float32, mybir.dt.bfloat16, mybir.dt.uint16
mult, add, largest = mybir.AluOpType.mult, mybir.AluOpType.add, mybir.AluOpType.max
tanh = mybir.ActivationFunctionType.Tanh
relu = mybir.ActivationFunctionType.Relu

P = 128
K, S, N, M = 256, 2048, 512, 128
BLOCKS = K // P
PIECES = 4
C = N // PIECES

FLOPS = 2 * K * M * N + 2 * K * N


def tile_lookup_vg_multanh_relu_kernel(tc, tab, y, w, b, offs, out):
    nc = tc.nc
    with (
        tc.tile_pool(name="held", bufs=1) as held,
        tc.psum_pool(name="psum", bufs=1) as psum,
    ):
        offsets = held.tile([P, N // 16], U16, name="offsets")
        values = [held.tile([P, S], F32, name=f"values{k}") for k in range(BLOCKS)]
        gates = [held.tile([P, S], F32, name=f"gates{k}") for k in range(BLOCKS)]
        stream = held.tile([P, BLOCKS, N], F32, name="stream")
        weights = held.tile([P, BLOCKS, M], BF16, name="weights")
        bias = held.tile([P, 1], F32, name="bias")

        nc.scalar.dma_start(weights[:], w.rearrange("(k p) m -> p k m", p=P))
        nc.scalar.dma_start(bias[:], b)
        nc.sync.dma_start(offsets[:], offs)
        nc.sync.dma_start(gates[0][:], tab[1, 0:P, :])
        nc.sync.dma_start(stream[:, 0, :], y[0:P, :])
        nc.sync.dma_start(values[0][:], tab[0, 0:P, :])
        nc.sync.dma_start(stream[:, 1, :], y[P:K, :])
        nc.sync.dma_start(values[1][:], tab[0, P:K, :])
        nc.sync.dma_start(gates[1][:], tab[1, P:K, :])

        layer = [psum.tile([M, C], F32, name=f"layer{c}") for c in range(PIECES)]
        for k in range(BLOCKS):
            scaled = [held.tile([P, C], F32, name=f"scaled{k}_{c}") for c in range(PIECES)]
            gate = [held.tile([P, C], F32, name=f"gate{k}_{c}") for c in range(PIECES)]
            x = [held.tile([P, C], BF16, name=f"x{k}_{c}") for c in range(PIECES)]
            for c in range(PIECES):
                entries = offsets[:, c * C // 16 : (c + 1) * C // 16]
                nc.vector.tensor_tensor(
                    scaled[c][:], values[k][:].indirect(entries), stream[:, k, c * C : (c + 1) * C], mult
                )
            for c in range(PIECES):
                entries = offsets[:, c * C // 16 : (c + 1) * C // 16]
                nc.scalar.activation(gate[c][:], gates[k][:].indirect(entries), tanh)
                nc.vector.tensor_tensor(x[c][:], scaled[c][:], gate[c][:], mult)
                nc.tensor.matmul(layer[c][:], weights[:, k, :], x[c][:], start=k == 0, stop=k == BLOCKS - 1)

        for c in range(PIECES):
            result = held.tile([M, C], F32, name=f"result{c}")
            if c % 2 == 0:
                nc.scalar.activation(result[:], layer[c][:], relu, bias=bias[:])
            else:
                nc.vector.tensor_scalar(result[:], layer[c][:], bias[:], 0.0, add, largest)
            nc.sync.dma_start(out[:, c * C : (c + 1) * C], result[:])
